import numpy as np, ml_dtypes
CORES = [26,28,98,100,106,108,122,124]
N = 8
F = 32
BETA, LR = 0.75, 0.5
def setup_inputs(rng):
    return {"gr": rng.standard_normal((N, 128, N * F), dtype=np.float32).astype(ml_dtypes.bfloat16), "m": rng.standard_normal((N, 128, F), dtype=np.float32).astype(ml_dtypes.bfloat16), "w": rng.standard_normal((N, 128, F), dtype=np.float32).astype(ml_dtypes.bfloat16)}
def setup_inputs_big(rng):
    d = setup_inputs(rng)
    for k in ("gr", "m", "w"): d[k] = (d[k].astype(np.float32) * 1048576.0).astype(d[k].dtype)
    return d
def setup_inputs_small(rng):
    d = setup_inputs(rng)
    for k in ("gr", "m", "w"): d[k] = (d[k].astype(np.float32) * (1 / 1048576.0)).astype(d[k].dtype)
    return d
def setup_inputs_apart(rng):
    d = setup_inputs(rng)
    f = (10.0 ** rng.permutation(np.linspace(-1.5, 1.5, N))).astype(np.float32).reshape(N, 1, 1)
    for k in ("gr", "m", "w"): d[k] = (d[k].astype(np.float32) * f).astype(d[k].dtype)
    return d
def reference(gr, m, w):
    GR, M, W = gr.astype(np.float64), m.astype(np.float64), w.astype(np.float64)
    s = GR.sum(axis=0)
    m2 = np.stack([BETA * M[r] + s[:, F * r:F * r + F] for r in range(N)])
    w2 = np.concatenate([W[r] - LR * m2[r] for r in range(N)], axis=1)
    return {"y": np.broadcast_to(w2.astype(ml_dtypes.bfloat16), (N, 128, N * F)), "mo": m2.astype(ml_dtypes.bfloat16)}

@@ -1,0 +1,142 @@
+from concourse.bass import DstId, RemoteDMATransfer
+from concourse.mybir import AluOpType
+
+F = 32
+COLS = 256
+HALF = 128
+
+SCRATCH = {
+    "G": ("sbuf", [128, COLS], "bfloat16"),
+    "M": ("sbuf", [128, F], "bfloat16"),
+    "W": ("sbuf", [128, F], "bfloat16"),
+    "c75": ("sbuf", [128, F], "bfloat16"),
+    "t1": ("sbuf", [128, F], "bfloat16"),
+    "w2": ("sbuf", [128, F], "bfloat16"),
+    "v": ("sbuf", [128, F], "bfloat16"),
+    "S": ("sbuf", [128, COLS], "bfloat16"),
+    "Y": ("sbuf", [128, COLS], "bfloat16"),
+    "MO": ("sbuf", [128, F], "bfloat16"),
+    "ch": ("psum", [128, COLS], "float32"),
+    "hin": ("dram", [2, 128, HALF], "bfloat16"),
+    "rin": ("dram", [4, 128, HALF], "bfloat16"),
+}
+SEMAPHORES = ["ldg", "ldmw", "vc", "va", "vb", "gready", "lsem", "hsem", "rsem", "s0", "s1", "vmo", "vy0", "vy1", "st"]
+
+
+def _bits(mask):
+    return [1 << i for i in range(mask.bit_length()) if (mask >> i) & 1]
+
+
+def _plan(T, topo):
+    ranks = list(T.cores)
+    chips = []
+    for c in ranks:
+        if topo.chip(c) not in chips:
+            chips.append(topo.chip(c))
+    on_chip = {x: [c for c in ranks if topo.chip(c) == x] for x in chips}
+    helpers = {}
+    for x in chips:
+        by_die = {}
+        for c in range(topo.CORES_PER_CHIP * topo.CHIPS):
+            if topo.chip(c) != x or c in ranks:
+                continue
+            if all(topo.may_write(c, d) for d in ranks):
+                by_die.setdefault(topo.die(c), c)
+        helpers[x] = [by_die[d] for d in sorted(by_die)]
+    return chips, on_chip, helpers
+
+
+def _dst(topo, c):
+    rid, pid, _ = topo.addr(c)
+    return DstId(rid=rid, pnc=pid)
+
+
+def rank_program(g, core, T, topo):
+    chips, on_chip, helpers = _plan(T, topo)
+    x = topo.chip(core)
+    if x not in chips:
+        return
+    sem = T.sem
+    rank = T.rank_of(core)
+
+    if rank is None:
+        if core not in helpers[x]:
+            return
+        h = helpers[x].index(core)
+        xi = chips.index(x)
+        mine = on_chip[x]
+        peers = [helpers[y][h] for y in chips if y != x]
+        n1 = len(_bits(topo.mask(mine[0], core))) // 2
+        m2 = topo.mask(core, peers[0])
+        for p in peers:
+            m2 &= topo.mask(core, p)
+        n2 = len(_bits(m2))
+        g.wait_ge(sem.hsem, n1 * len(mine))
+        g.remote_dma_fused([RemoteDMATransfer(
+            dst_ids=[_dst(topo, p) for p in peers], dma_engine_mask=m2, remote_sem=sem.rsem,
+            srcs=[T.hin[0], T.hin[1]], dsts=[T.rin[xi] for p in peers], alu_op=1)], local_sem=sem.lsem)
+        m3 = topo.mask(core, mine[0])
+        for r in mine:
+            m3 &= topo.mask(core, r)
+        n3 = len(_bits(m3))
+        g.wait_ge(sem.rsem, n2 * len(peers))
+        g.remote_dma_fused([RemoteDMATransfer(
+            dst_ids=[_dst(topo, r) for r in mine], dma_engine_mask=m3, remote_sem=sem["s%d" % h],
+            srcs=[T.hin[0], T.hin[1]] + [T.rin[i] for i in range(len(chips)) if i != xi],
+            dsts=[T.S[:, h * HALF:(h + 1) * HALF] for r in mine], alu_op=1)], local_sem=sem.lsem)
+        g.wait_ge(sem.lsem, n2 + n3)
+        return
+
+    s = on_chip[x].index(core)
+    blk = slice(rank * F, (rank + 1) * F)
+    own = (rank * F) // HALF
+    oth = 1 - own
+    V = g.vector
+
+    g.sync.dma_start(T.G[:], T.gr[:]).then_inc(sem.ldg, 16)
+    g.scalar.dma_start(T.W[:], T.w[:]).then_inc(sem.ldmw, 16)
+    g.scalar.dma_start(T.M[:], T.m[:]).then_inc(sem.ldmw, 16)
+
+    V.memset(T.c75[:], 0.75).then_inc(sem.vc, 1)
+    V.memset(T.ch[:], -0.5).then_inc(sem.vc, 1)
+    V.wait_ge(sem.vc, 2)
+    V.wait_ge(sem.ldmw, 32)
+    V.tensor_tensor(T.w2[:], T.W[:], T.W[:], AluOpType.add).then_inc(sem.va, 1)
+    V.tensor_tensor(T.t1[:], T.M[:], T.c75[:], AluOpType.mult).then_inc(sem.va, 1)
+    V.wait_ge(sem.va, 2)
+    V.tensor_tensor(T.v[:], T.t1[:], T.w2[:], AluOpType.subtract).then_inc(sem.vb, 1)
+    V.wait_ge(sem.vb, 1)
+    V.wait_ge(sem.ldg, 16)
+    V.tensor_tensor(T.G[:, blk], T.G[:, blk], T.v[:], AluOpType.add).then_inc(sem.gready, 1)
+
+    hs = helpers[x]
+    trs = []
+    n_loc = 0
+    for h, hc in enumerate(hs):
+        b = _bits(topo.mask(core, hc))
+        k = len(b) // len(hs)
+        trs.append(RemoteDMATransfer(
+            dst_ids=[_dst(topo, hc)], dma_engine_mask=sum(b[h * k:(h + 1) * k]), remote_sem=sem.hsem,
+            src=T.G[:, h * HALF:(h + 1) * HALF], dst=T.hin[s]))
+        n_loc += k
+    g.wait_ge(sem.gready, 1)
+    g.remote_dma_fused(trs, local_sem=sem.lsem)
+
+    n3 = [len(_bits(topo.mask(hc, core))) for hc in hs]
+    co = slice(own * HALF, (own + 1) * HALF)
+    ct = slice(oth * HALF, (oth + 1) * HALF)
+    V.wait_ge(sem["s%d" % own], n3[own])
+    V.tensor_tensor(T.MO[:], T.S[:, blk], T.w2[:], AluOpType.add).then_inc(sem.vmo, 1)
+    V.tensor_tensor(T.Y[:, co], T.S[:, co], T.ch[:, co], AluOpType.mult).then_inc(sem.vy0, 1)
+    V.wait_ge(sem["s%d" % oth], n3[oth])
+    V.tensor_tensor(T.Y[:, ct], T.S[:, ct], T.ch[:, ct], AluOpType.mult).then_inc(sem.vy1, 1)
+
+    g.sync.wait_ge(sem.vmo, 1)
+    g.sync.dma_start(T.mo[:], T.MO[:]).then_inc(sem.st, 16)
+    g.scalar.wait_ge(sem.vy0, 1)
+    g.scalar.dma_start(T.y[:, co], T.Y[:, co]).then_inc(sem.st, 16)
+    g.sync.wait_ge(sem.vy1, 1)
+    g.sync.dma_start(T.y[:, ct], T.Y[:, ct]).then_inc(sem.st, 16)
+
+    g.wait_ge(sem.lsem, n_loc)
+    g.wait_ge(sem.st, 48)

@@ -12,7 +12,7 @@ SCRATCH = {
     "c75": ("sbuf", [128, F], "bfloat16"),
     "t1": ("sbuf", [128, F], "bfloat16"),
     "w2": ("sbuf", [128, F], "bfloat16"),
-    "v": ("sbuf", [128, F], "bfloat16"),
+    "X": ("sbuf", [128, F], "bfloat16"),
     "S": ("sbuf", [128, COLS], "bfloat16"),
     "Y": ("sbuf", [128, COLS], "bfloat16"),
     "MO": ("sbuf", [128, F], "bfloat16"),
@@ -20,7 +20,8 @@ SCRATCH = {
     "hin": ("dram", [2, 128, HALF], "bfloat16"),
     "rin": ("dram", [4, 128, HALF], "bfloat16"),
 }
-SEMAPHORES = ["ldg", "ldmw", "vc", "va", "vb", "gready", "lsem", "hsem", "rsem", "s0", "s1", "vmo", "vy0", "vy1", "st"]
+SEMAPHORES = ["ldg", "ldw", "ldm", "vc", "va", "vb", "gready", "lsem", "hsem", "rsem", "s0", "s1",
+              "vmo", "vy0", "vy1", "st"]
 
 
 def _bits(mask):
@@ -51,6 +52,20 @@ def _dst(topo, c):
     return DstId(rid=rid, pnc=pid)
 
 
+def _hop1_masks(topo, core, hs):
+    return [topo.mask(core, hc) for hc in hs]
+
+
+def _helper_masks(topo, hc, peers, mine):
+    m2 = topo.mask(hc, peers[0])
+    for p in peers:
+        m2 &= topo.mask(hc, p)
+    m3 = topo.mask(hc, mine[0])
+    for r in mine:
+        m3 &= topo.mask(hc, r)
+    return m2, m3
+
+
 def rank_program(g, core, T, topo):
     chips, on_chip, helpers = _plan(T, topo)
     x = topo.chip(core)
@@ -58,27 +73,22 @@ def rank_program(g, core, T, topo):
         return
     sem = T.sem
     rank = T.rank_of(core)
+    mine = on_chip[x]
+    hs = helpers[x]
 
     if rank is None:
-        if core not in helpers[x]:
+        if core not in hs:
             return
-        h = helpers[x].index(core)
+        h = hs.index(core)
         xi = chips.index(x)
-        mine = on_chip[x]
         peers = [helpers[y][h] for y in chips if y != x]
-        n1 = len(_bits(topo.mask(mine[0], core))) // 2
-        m2 = topo.mask(core, peers[0])
-        for p in peers:
-            m2 &= topo.mask(core, p)
-        n2 = len(_bits(m2))
-        g.wait_ge(sem.hsem, n1 * len(mine))
+        n1 = sum(len(_bits(_hop1_masks(topo, r, hs)[h])) for r in mine)
+        m2, m3 = _helper_masks(topo, core, peers, mine)
+        n2, n3 = len(_bits(m2)), len(_bits(m3))
+        g.wait_ge(sem.hsem, n1)
         g.remote_dma_fused([RemoteDMATransfer(
             dst_ids=[_dst(topo, p) for p in peers], dma_engine_mask=m2, remote_sem=sem.rsem,
             srcs=[T.hin[0], T.hin[1]], dsts=[T.rin[xi] for p in peers], alu_op=1)], local_sem=sem.lsem)
-        m3 = topo.mask(core, mine[0])
-        for r in mine:
-            m3 &= topo.mask(core, r)
-        n3 = len(_bits(m3))
         g.wait_ge(sem.rsem, n2 * len(peers))
         g.remote_dma_fused([RemoteDMATransfer(
             dst_ids=[_dst(topo, r) for r in mine], dma_engine_mask=m3, remote_sem=sem["s%d" % h],
@@ -87,42 +97,44 @@ def rank_program(g, core, T, topo):
         g.wait_ge(sem.lsem, n2 + n3)
         return
 
-    s = on_chip[x].index(core)
+    s = mine.index(core)
     blk = slice(rank * F, (rank + 1) * F)
     own = (rank * F) // HALF
     oth = 1 - own
     V = g.vector
 
     g.sync.dma_start(T.G[:], T.gr[:]).then_inc(sem.ldg, 16)
-    g.scalar.dma_start(T.W[:], T.w[:]).then_inc(sem.ldmw, 16)
-    g.scalar.dma_start(T.M[:], T.m[:]).then_inc(sem.ldmw, 16)
+    g.scalar.dma_start(T.W[:], T.w[:]).then_inc(sem.ldw, 16)
+    g.scalar.dma_start(T.M[:], T.m[:]).then_inc(sem.ldm, 16)
+
+    m1 = _hop1_masks(topo, core, hs)
+
+    def send(h):
+        g.remote_dma_fused([RemoteDMATransfer(
+            dst_ids=[_dst(topo, hs[h])], dma_engine_mask=m1[h], remote_sem=sem.hsem,
+            src=T.G[:, h * HALF:(h + 1) * HALF], dst=T.hin[s])], local_sem=sem.lsem)
+
+    g.wait_ge(sem.ldg, 16)
+    send(oth)
 
     V.memset(T.c75[:], 0.75).then_inc(sem.vc, 1)
     V.memset(T.ch[:], -0.5).then_inc(sem.vc, 1)
     V.wait_ge(sem.vc, 2)
-    V.wait_ge(sem.ldmw, 32)
+    V.wait_ge(sem.ldw, 16)
     V.tensor_tensor(T.w2[:], T.W[:], T.W[:], AluOpType.add).then_inc(sem.va, 1)
-    V.tensor_tensor(T.t1[:], T.M[:], T.c75[:], AluOpType.mult).then_inc(sem.va, 1)
-    V.wait_ge(sem.va, 2)
-    V.tensor_tensor(T.v[:], T.t1[:], T.w2[:], AluOpType.subtract).then_inc(sem.vb, 1)
-    V.wait_ge(sem.vb, 1)
+    V.wait_ge(sem.va, 1)
     V.wait_ge(sem.ldg, 16)
-    V.tensor_tensor(T.G[:, blk], T.G[:, blk], T.v[:], AluOpType.add).then_inc(sem.gready, 1)
+    V.tensor_tensor(T.X[:], T.G[:, blk], T.w2[:], AluOpType.subtract).then_inc(sem.vb, 1)
+    V.wait_ge(sem.ldm, 16)
+    V.tensor_tensor(T.t1[:], T.M[:], T.c75[:], AluOpType.mult).then_inc(sem.vb, 1)
+    V.wait_ge(sem.vb, 2)
+    V.tensor_tensor(T.G[:, blk], T.X[:], T.t1[:], AluOpType.add).then_inc(sem.gready, 1)
 
-    hs = helpers[x]
-    trs = []
-    n_loc = 0
-    for h, hc in enumerate(hs):
-        b = _bits(topo.mask(core, hc))
-        k = len(b) // len(hs)
-        trs.append(RemoteDMATransfer(
-            dst_ids=[_dst(topo, hc)], dma_engine_mask=sum(b[h * k:(h + 1) * k]), remote_sem=sem.hsem,
-            src=T.G[:, h * HALF:(h + 1) * HALF], dst=T.hin[s]))
-        n_loc += k
     g.wait_ge(sem.gready, 1)
-    g.remote_dma_fused(trs, local_sem=sem.lsem)
+    send(own)
 
-    n3 = [len(_bits(topo.mask(hc, core))) for hc in hs]
+    n3 = [len(_bits(_helper_masks(topo, hc, [helpers[y][h] for y in chips if y != x], mine)[1]))
+          for h, hc in enumerate(hs)]
     co = slice(own * HALF, (own + 1) * HALF)
     ct = slice(oth * HALF, (oth + 1) * HALF)
     V.wait_ge(sem["s%d" % own], n3[own])
@@ -138,5 +150,5 @@ def rank_program(g, core, T, topo):
     g.sync.wait_ge(sem.vy1, 1)
     g.sync.dma_start(T.y[:, ct], T.Y[:, ct]).then_inc(sem.st, 16)
 
-    g.wait_ge(sem.lsem, n_loc)
+    g.wait_ge(sem.lsem, sum(len(_bits(m)) for m in m1))
     g.wait_ge(sem.st, 48)

from concourse.bass import DstId, RemoteDMATransfer
from concourse.mybir import AluOpType

F = 32
COLS = 256
HALF = 128

SCRATCH = {
    "G": ("sbuf", [128, COLS], "bfloat16"),
    "M": ("sbuf", [128, F], "bfloat16"),
    "W": ("sbuf", [128, F], "bfloat16"),
    "c75": ("sbuf", [128, F], "bfloat16"),
    "t1": ("sbuf", [128, F], "bfloat16"),
    "w2": ("sbuf", [128, F], "bfloat16"),
    "X": ("sbuf", [128, F], "bfloat16"),
    "S": ("sbuf", [128, COLS], "bfloat16"),
    "Y": ("sbuf", [128, COLS], "bfloat16"),
    "MO": ("sbuf", [128, F], "bfloat16"),
    "ch": ("psum", [128, COLS], "float32"),
    "hin": ("dram", [2, 128, HALF], "bfloat16"),
    "rin": ("dram", [4, 128, HALF], "bfloat16"),
}
SEMAPHORES = ["ldg", "ldw", "ldm", "vc", "va", "vb", "gready", "lsem", "hsem", "rsem", "s0", "s1",
              "vmo", "vy0", "vy1", "st"]


def _bits(mask):
    return [1 << i for i in range(mask.bit_length()) if (mask >> i) & 1]


def _plan(T, topo):
    ranks = list(T.cores)
    chips = []
    for c in ranks:
        if topo.chip(c) not in chips:
            chips.append(topo.chip(c))
    on_chip = {x: [c for c in ranks if topo.chip(c) == x] for x in chips}
    helpers = {}
    for x in chips:
        by_die = {}
        for c in range(topo.CORES_PER_CHIP * topo.CHIPS):
            if topo.chip(c) != x or c in ranks:
                continue
            if all(topo.may_write(c, d) for d in ranks):
                by_die.setdefault(topo.die(c), c)
        helpers[x] = [by_die[d] for d in sorted(by_die)]
    return chips, on_chip, helpers


def _dst(topo, c):
    rid, pid, _ = topo.addr(c)
    return DstId(rid=rid, pnc=pid)


def _hop1_masks(topo, core, hs):
    return [topo.mask(core, hc) for hc in hs]


def _helper_masks(topo, hc, peers, mine):
    m2 = topo.mask(hc, peers[0])
    for p in peers:
        m2 &= topo.mask(hc, p)
    m3 = topo.mask(hc, mine[0])
    for r in mine:
        m3 &= topo.mask(hc, r)
    return m2, m3


def rank_program(g, core, T, topo):
    chips, on_chip, helpers = _plan(T, topo)
    x = topo.chip(core)
    if x not in chips:
        return
    sem = T.sem
    rank = T.rank_of(core)
    mine = on_chip[x]
    hs = helpers[x]

    if rank is None:
        if core not in hs:
            return
        h = hs.index(core)
        xi = chips.index(x)
        peers = [helpers[y][h] for y in chips if y != x]
        n1 = sum(len(_bits(_hop1_masks(topo, r, hs)[h])) for r in mine)
        m2, m3 = _helper_masks(topo, core, peers, mine)
        n2, n3 = len(_bits(m2)), len(_bits(m3))
        g.wait_ge(sem.hsem, n1)
        g.remote_dma_fused([RemoteDMATransfer(
            dst_ids=[_dst(topo, p) for p in peers], dma_engine_mask=m2, remote_sem=sem.rsem,
            srcs=[T.hin[0], T.hin[1]], dsts=[T.rin[xi] for p in peers], alu_op=1)], local_sem=sem.lsem)
        g.wait_ge(sem.rsem, n2 * len(peers))
        g.remote_dma_fused([RemoteDMATransfer(
            dst_ids=[_dst(topo, r) for r in mine], dma_engine_mask=m3, remote_sem=sem["s%d" % h],
            srcs=[T.hin[0], T.hin[1]] + [T.rin[i] for i in range(len(chips)) if i != xi],
            dsts=[T.S[:, h * HALF:(h + 1) * HALF] for r in mine], alu_op=1)], local_sem=sem.lsem)
        g.wait_ge(sem.lsem, n2 + n3)
        return

    s = mine.index(core)
    blk = slice(rank * F, (rank + 1) * F)
    own = (rank * F) // HALF
    oth = 1 - own
    V = g.vector

    g.sync.dma_start(T.G[:], T.gr[:]).then_inc(sem.ldg, 16)
    g.scalar.dma_start(T.W[:], T.w[:]).then_inc(sem.ldw, 16)
    g.scalar.dma_start(T.M[:], T.m[:]).then_inc(sem.ldm, 16)

    m1 = _hop1_masks(topo, core, hs)

    def send(h):
        g.remote_dma_fused([RemoteDMATransfer(
            dst_ids=[_dst(topo, hs[h])], dma_engine_mask=m1[h], remote_sem=sem.hsem,
            src=T.G[:, h * HALF:(h + 1) * HALF], dst=T.hin[s])], local_sem=sem.lsem)

    g.wait_ge(sem.ldg, 16)
    send(oth)

    V.memset(T.c75[:], 0.75).then_inc(sem.vc, 1)
    V.memset(T.ch[:], -0.5).then_inc(sem.vc, 1)
    V.wait_ge(sem.vc, 2)
    V.wait_ge(sem.ldw, 16)
    V.tensor_tensor(T.w2[:], T.W[:], T.W[:], AluOpType.add).then_inc(sem.va, 1)
    V.wait_ge(sem.va, 1)
    V.wait_ge(sem.ldg, 16)
    V.tensor_tensor(T.X[:], T.G[:, blk], T.w2[:], AluOpType.subtract).then_inc(sem.vb, 1)
    V.wait_ge(sem.ldm, 16)
    V.tensor_tensor(T.t1[:], T.M[:], T.c75[:], AluOpType.mult).then_inc(sem.vb, 1)
    V.wait_ge(sem.vb, 2)
    V.tensor_tensor(T.G[:, blk], T.X[:], T.t1[:], AluOpType.add).then_inc(sem.gready, 1)

    g.wait_ge(sem.gready, 1)
    send(own)

    n3 = [len(_bits(_helper_masks(topo, hc, [helpers[y][h] for y in chips if y != x], mine)[1]))
          for h, hc in enumerate(hs)]
    co = slice(own * HALF, (own + 1) * HALF)
    ct = slice(oth * HALF, (oth + 1) * HALF)
    V.wait_ge(sem["s%d" % own], n3[own])
    V.tensor_tensor(T.MO[:], T.S[:, blk], T.w2[:], AluOpType.add).then_inc(sem.vmo, 1)
    V.tensor_tensor(T.Y[:, co], T.S[:, co], T.ch[:, co], AluOpType.mult).then_inc(sem.vy0, 1)
    V.wait_ge(sem["s%d" % oth], n3[oth])
    V.tensor_tensor(T.Y[:, ct], T.S[:, ct], T.ch[:, ct], AluOpType.mult).then_inc(sem.vy1, 1)

    g.sync.wait_ge(sem.vmo, 1)
    g.sync.dma_start(T.mo[:], T.MO[:]).then_inc(sem.st, 16)
    g.scalar.wait_ge(sem.vy0, 1)
    g.scalar.dma_start(T.y[:, co], T.Y[:, co]).then_inc(sem.st, 16)
    g.sync.wait_ge(sem.vy1, 1)
    g.sync.dma_start(T.y[:, ct], T.Y[:, ct]).then_inc(sem.st, 16)

    g.wait_ge(sem.lsem, sum(len(_bits(m)) for m in m1))
    g.wait_ge(sem.st, 48)
